import numpy as np
import ml_dtypes


def mxq(x, axis, fmt="e4m3"):
    dtype, down = {"e4m3": (ml_dtypes.float8_e4m3fn, 7), "e5m2": (ml_dtypes.float8_e5m2, 14)}[fmt]
    v = np.moveaxis(np.asarray(x, np.float32).astype(ml_dtypes.bfloat16).astype(np.float64), axis, -1)
    blocks = v.reshape(v.shape[:-1] + (-1, 32))
    amax = np.abs(blocks).max(-1, keepdims=True)
    byte = np.maximum(np.where(amax > 0, np.frexp(amax)[1] - 1 + 127, 0) - down, 1)
    scale = np.exp2(byte - 127.0)
    codes = (blocks / scale).astype(np.float32).astype(dtype).astype(np.float64)
    return np.moveaxis((codes * scale).reshape(v.shape), -1, axis)


WIDE = False


def mx_kscale(k):
    if not WIDE:
        return np.ones(k)
    levels = np.array([30, -30])
    if k % 512:
        return np.exp2(np.random.permutation(np.resize(levels, k // 32))).repeat(32)
    a = np.empty((k // 512, 16))
    for p in range(k // 512):
        a[p, :8] = np.random.permutation(np.resize(levels, 8))
        for g in range(8):
            far = levels[np.abs(levels - a[p, g]) >= 10]
            a[p, g + 8] = far[np.random.randint(len(far))]
    return np.exp2(a.ravel()).repeat(32)


def f64(x):
    return np.asarray(x).astype(np.float64)


def striped(idx):
    return np.tile(np.asarray(idx).reshape(-1, 16).T, (8, 1)).astype(np.uint16)


def unstriped(offs):
    return offs[:16].T.reshape(-1).astype(np.int64)


E2M1 = np.array([0.0, 0.5, 1.0, 1.5, 2.0, 3.0, 4.0, 6.0, -0.0, -0.5, -1.0, -1.5, -2.0, -3.0, -4.0, -6.0])


def pack_weight(w, fmt):
    k, n = w.shape
    w = f64(np.asarray(w, np.float32).astype(ml_dtypes.bfloat16)).reshape(k // 32, 32, n)
    amax = np.abs(w).max(1)
    if fmt in ("e4m3", "e5m2"):
        byte = np.frexp(amax)[1] - 1 + 127 - (7 if fmt == "e4m3" else 14)
    else:
        mant, ex = np.frexp(amax / 6.0)
        byte = np.where(mant > 0.5, ex, ex - 1) + 127
    byte = np.clip(np.where(amax > 0, byte, 1), 1, 254)
    scaled = (w * np.exp2(127.0 - byte)[:, None, :]).reshape(k, n).astype(np.float32)
    by_word = np.ascontiguousarray(scaled.reshape(k // 512, 128, 4, n).transpose(0, 1, 3, 2))
    if fmt in ("e4m3", "e5m2"):
        words = by_word.astype(ml_dtypes.float8_e4m3fn if fmt == "e4m3" else ml_dtypes.float8_e5m2).view(np.uint8)
    else:
        c = by_word.astype(ml_dtypes.float4_e2m1fn).view(np.uint8) & 0xF
        words = (c[..., 0::2] | (c[..., 1::2] << 4)).reshape(k // 512, 128, 2 * n)
    return np.ascontiguousarray(words), np.ascontiguousarray(byte.astype(np.uint8).reshape(k // 512, 16, n))


def unpack_weight(words, scales, fmt):
    g, _, n = scales.shape
    words = np.ascontiguousarray(words).reshape(g, 128, n, -1)
    if fmt in ("e4m3", "e5m2"):
        vals = words.view(ml_dtypes.float8_e4m3fn if fmt == "e4m3" else ml_dtypes.float8_e5m2).astype(np.float64)
    else:
        nib = np.empty((g, 128, n, 4), np.uint8)
        nib[..., 0::2] = words & 0xF
        nib[..., 1::2] = words >> 4
        vals = E2M1[nib]
    vals = vals * np.repeat(np.exp2(scales.astype(np.float64) - 127.0), 8, axis=1)[..., None]
    return vals.transpose(0, 1, 3, 2).reshape(g * 512, n)


K, T, J, R, O, N = 1024, 1024, 256, 512, 128, 256


def setup_inputs():
    n = np.random.standard_normal
    idx = np.random.permutation(T)[:J]
    idx2 = np.random.permutation(T)[:J]
    idx3 = np.random.permutation(J)[:O]
    fk = mx_kscale(K)
    fr = mx_kscale(R)
    wp = pack_weight(n((K, R)) * 1 / np.sqrt(K) * fk[:, None] * fr, "e5m2")
    wbp = pack_weight(n((R, N)) * 1 / np.sqrt(R) / fr[:, None], "e2m1")
    return {
        "xf": (n((K, T))).astype(np.float32),
        "fk": (np.random.uniform(0.5, 2.0, (K, 1)) / fk[:, None]).astype(np.float32),
        "w_words": wp[0],
        "w_scales": wp[1],
        "wb_words": wbp[0],
        "wb_scales": wbp[1],
        "rs": (1.0 * n((O, N))).astype(np.float32),
        "offs": striped(idx),
        "offs2": striped(idx2),
        "offs3": striped(idx3),
    }


def reference(xf, fk, w_words, w_scales, wb_words, wb_scales, rs, offs, offs2, offs3):
    idx = unstriped(offs)
    idx2 = unstriped(offs2)
    idx3 = unstriped(offs3)
    wu = unpack_weight(w_words, w_scales, "e5m2")
    wbu = unpack_weight(wb_words, wb_scales, "e2m1")
    u = np.maximum(f64(xf)[:, idx], f64(xf)[:, idx2]) * f64(fk)
    uq = mxq(u, 0, "e5m2")
    a = wu.T @ uq
    ha = np.maximum(a, 0.0)
    hid = ha[:, idx3]
    hidq = mxq(hid, 0, "e5m2")
    p = hidq.T @ wbu
    pk2 = np.max(np.abs(p), axis=1, keepdims=True)
    y = p / (pk2 + 0.2) + 0.3 * f64(rs)
    return y

@@ -1,0 +1,205 @@
+from contextlib import ExitStack
+
+import concourse.mybir as mybir
+
+K, T, J, R, O, N = 1024, 1024, 256, 512, 128, 256
+FLOPS = 2 * K * R * J + 2 * R * O * N
+
+F32 = mybir.dt.float32
+BF16 = mybir.dt.bfloat16
+I32 = mybir.dt.int32
+U16 = mybir.dt.uint16
+U8 = mybir.dt.uint8
+E5M2X4 = mybir.dt.float8_e5m2_x4
+E2M1X4 = mybir.dt.float4_e2m1fn_x4
+ALU = mybir.AluOpType
+ACT = mybir.ActivationFunctionType
+
+P = 128
+PACK = 4
+PASSES = K // (P * PACK)
+HALF = J // 2
+LINE = 4
+
+
+def tile_list_largerpicks_relooked_rowpeaks_kernel(
+    tc, xf, fk, w_words, w_scales, wb_words, wb_scales, rs, offs, offs2, offs3, out
+):
+    nc = tc.nc
+    with ExitStack() as ctx:
+        keep = ctx.enter_context(tc.tile_pool(name="keep", bufs=1))
+        psum = ctx.enter_context(tc.psum_pool(name="psum", bufs=1))
+
+        list1 = keep.tile([P, J // 16], U16, name="list1")
+        list2 = keep.tile([P, J // 16], U16, name="list2")
+        list3 = keep.tile([P, O // 16], U16, name="list3")
+        planes = [[keep.tile([P, T], F32, name=f"x{z}{t}") for t in range(PACK)] for z in range(PASSES)]
+        factor = keep.tile([P, PASSES, PACK], F32, name="factor")
+        w_raw = [keep.tile([P, R], I32, name=f"w_raw{z}") for z in range(PASSES)]
+        w_codes = [keep.tile([P, R], I32, name=f"w_codes{z}", align_bytes=64) for z in range(PASSES)]
+        ws_raw = keep.tile([P, PASSES, R], U8, name="ws_raw")
+        ws = keep.tile([P, PASSES, R], U8, name="ws", align_bytes=64)
+        wb = keep.tile([P, 2 * N], U8, name="wb", align_bytes=64)
+        wbs = keep.tile([P, N], U8, name="wbs", align_bytes=64)
+        res = keep.tile([P, N], F32, name="res")
+
+        xv = xf.rearrange("(z p t) c -> z t p c", z=PASSES, t=PACK)
+
+        def load_plane(z, t):
+            nc.sync.dma_start(out=planes[z][t][:], in_=xv[z, t])
+
+        def load_w(z):
+            nc.sync.dma_start(out=w_raw[z][:], in_=w_words[z].rearrange("p c t -> p (c t)").bitcast(I32))
+
+        nc.vector.memset(ws_raw[:].rearrange("p z c -> p (z c)").bitcast(I32), 0)
+        nc.vector.memset(wbs[:].bitcast(I32), 0)
+
+        load_plane(0, 0)
+        nc.sync.dma_start(list1[:], offs)
+        nc.sync.dma_start(list2[:], offs2)
+        nc.sync.dma_start(out=factor[:], in_=fk.rearrange("(z p t) o -> p z (t o)", z=PASSES, t=PACK))
+        load_w(0)
+        load_plane(0, 1)
+        load_w(1)
+        load_plane(0, 2)
+        for q in range(4):
+            nc.sync.dma_start(
+                out=ws_raw[32 * q : 32 * q + 4].bitcast(I32),
+                in_=w_scales[:, 4 * q : 4 * q + 4, :].rearrange("z r c -> r z c").bitcast(I32),
+            )
+        load_plane(0, 3)
+        for t in range(PACK):
+            load_plane(1, t)
+        nc.sync.dma_start(list3[:], offs3)
+        nc.sync.dma_start(out=wb[:].bitcast(I32), in_=wb_words[0].bitcast(I32))
+        nc.sync.dma_start(out=res[:], in_=rs)
+        for q in range(4):
+            nc.sync.dma_start(
+                out=wbs[32 * q : 32 * q + 4].bitcast(I32),
+                in_=wb_scales[0, 4 * q : 4 * q + 4, :].bitcast(I32),
+            )
+
+        def gather(engine, dst, window, offsets):
+            if engine == "scalar":
+                nc.scalar.activation(dst, window.indirect(offsets), ACT.Copy)
+            else:
+                nc.vector.tensor_copy(dst, window.indirect(offsets))
+
+        def deal_w(z):
+            nc.vector.tensor_copy(
+                out=w_codes[z][:].rearrange("p (t c i) -> p c t i", t=PACK, i=LINE),
+                in_=w_raw[z][:].rearrange("p (c i t) -> p c t i", t=PACK, i=LINE),
+            )
+
+        u = [keep.tile([P, J, PACK], BF16, name=f"u{z}", align_bytes=64) for z in range(PASSES)]
+        u_codes = [keep.tile([P, J], I32, name=f"u_codes{z}", align_bytes=64) for z in range(PASSES)]
+        u_scales = [keep.tile([P, J], U8, name=f"u_scales{z}", align_bytes=64) for z in range(PASSES)]
+
+        def quantise_u(z, cols):
+            nc.vector.quantize_mx(
+                out=u_codes[z][:, cols].bitcast(E5M2X4),
+                scales=u_scales[z][:, cols],
+                in_=u[z][:, cols, :].rearrange("p j t -> p (j t)"),
+            )
+
+        halves = [slice(h * HALF, (h + 1) * HALF) for h in range(2)]
+        entries = [slice(h * HALF // 16, (h + 1) * HALF // 16) for h in range(2)]
+
+        def plane_work(z, t, vector_halves):
+            first = keep.tile([P, J], F32, name=f"first{z}{t}")
+            second = keep.tile([P, J], F32, name=f"second{z}{t}")
+            larger = keep.tile([P, J], F32, name=f"larger{z}{t}")
+            for h in range(2):
+                gather("scalar", first[:, halves[h]], planes[z][t][:], list1[:, entries[h]])
+                gather("vector" if h < vector_halves else "scalar", second[:, halves[h]], planes[z][t][:], list2[:, entries[h]])
+            for h in range(2):
+                nc.vector.tensor_tensor(larger[:, halves[h]], first[:, halves[h]], second[:, halves[h]], ALU.max)
+                nc.vector.tensor_scalar(u[z][:, halves[h], t], larger[:, halves[h]], factor[:, z, t : t + 1], None, ALU.mult)
+
+        banks = [[psum.tile([P, 2, HALF], F32, name=f"a{h}{d}") for d in range(2)] for h in range(2)]
+
+        def first_stage(z, h):
+            for t in range(PACK):
+                rows = slice(t * P, (t + 1) * P)
+                nc.tensor.matmul_mx(
+                    out=banks[h][t // 2][:, t % 2, :],
+                    lhsT=w_codes[z][:, rows].bitcast(E5M2X4),
+                    lhsT_scale=ws[:, z, rows],
+                    rhs=u_codes[z][:, halves[h]].bitcast(E5M2X4),
+                    rhs_scale=u_scales[z][:, halves[h]],
+                    start=(z == 0 and t % 2 == 0),
+                    stop=(z == PASSES - 1 and t % 2 == 1),
+                )
+
+        plane_work(0, 0, 2)
+        deal_w(0)
+        plane_work(0, 1, 1)
+        deal_w(1)
+        plane_work(0, 2, 0)
+        nc.vector.tensor_copy(
+            out=ws[:].rearrange("p z (t m) -> p z t m", t=PACK),
+            in_=ws_raw[:].rearrange("p z (m t) -> p z t m", t=PACK),
+        )
+        plane_work(0, 3, 1)
+        quantise_u(0, slice(0, J))
+        for h in range(2):
+            first_stage(0, h)
+        plane_work(1, 0, 0)
+        for t in range(1, PACK):
+            plane_work(1, t, 1)
+        for h in range(2):
+            quantise_u(1, halves[h])
+
+        res3 = keep.tile([P, N], F32, name="res3")
+        nc.scalar.activation(res3[:], res[:], ACT.Copy, scale=0.3)
+
+        ha = [keep.tile([P, 2, J], F32, name=f"ha{d}") for d in range(2)]
+        for h in range(2):
+            first_stage(1, h)
+            for d in range(2):
+                if h == 0 and d == 1:
+                    nc.vector.tensor_scalar(ha[d][:, :, halves[h]], banks[h][d][:], 0.0, None, ALU.max)
+                else:
+                    nc.scalar.activation(ha[d][:, :, halves[h]], banks[h][d][:], ACT.Relu)
+
+        hid32 = keep.tile([P, PACK, O], F32, name="hid32")
+        for t in range(PACK):
+            gather("scalar" if t == PACK - 1 else "vector", hid32[:, t, :], ha[t // 2][:, t % 2, :], list3[:])
+
+        hid = keep.tile([P, O, PACK], BF16, name="hid", align_bytes=64)
+        h_codes = keep.tile([P, O], I32, name="h_codes", align_bytes=64)
+        h_scales = keep.tile([P, O], U8, name="h_scales", align_bytes=64)
+        places = [slice(h * O // 2, (h + 1) * O // 2) for h in range(2)]
+        for s in places:
+            nc.vector.tensor_copy(
+                out=hid[:, s, :].rearrange("p (c i) t -> p c t i", i=LINE),
+                in_=hid32[:, :, s].rearrange("p t (c i) -> p c t i", i=LINE),
+            )
+        for s in places:
+            nc.vector.quantize_mx(
+                out=h_codes[:, s].bitcast(E5M2X4),
+                scales=h_scales[:, s],
+                in_=hid[:, s, :].rearrange("p o t -> p (o t)"),
+            )
+
+        prod = psum.tile([P, N], F32, name="prod")
+        nc.tensor.matmul_mx(
+            out=prod[:],
+            lhsT=h_codes[:].bitcast(E5M2X4),
+            lhsT_scale=h_scales[:],
+            rhs=wb[:].bitcast(E2M1X4),
+            rhs_scale=wbs[:],
+            start=True,
+            stop=True,
+        )
+
+        size = keep.tile([P, N], F32, name="size")
+        shifted = keep.tile([P, N], F32, name="shifted")
+        peak = keep.tile([P, 1], F32, name="peak")
+        inverse = keep.tile([P, 1], F32, name="inverse")
+        result = keep.tile([P, N], F32, name="result")
+        nc.scalar.activation(size[:], prod[:], ACT.Abs)
+        nc.vector.tensor_scalar(shifted[:], size[:], 0.2, None, ALU.add, ALU.max, accum_out=peak[:])
+        nc.vector.reciprocal(inverse[:], peak[:])
+        nc.vector.scalar_tensor_tensor(result[:], prod[:], inverse[:], res3[:], ALU.mult, ALU.add)
+        nc.sync.dma_start(out=out, in_=result[:])

@@ -51,25 +51,36 @@ def tile_list_largerpicks_relooked_rowpeaks_kernel(
         def load_w(z):
             nc.sync.dma_start(out=w_raw[z][:], in_=w_words[z].rearrange("p c t -> p (c t)").bitcast(I32))
 
-        nc.vector.memset(ws_raw[:].rearrange("p z c -> p (z c)").bitcast(I32), 0)
-        nc.vector.memset(wbs[:].bitcast(I32), 0)
+        nc.gpsimd.memset(ws_raw[:].rearrange("p z c -> p (z c)").bitcast(I32), 0)
+        nc.gpsimd.memset(wbs[:].bitcast(I32), 0)
+        warm_in = keep.tile([P, 1], F32, name="warm_in")
+        warm_out = keep.tile([P, 1], F32, name="warm_out")
+        nc.vector.memset(warm_in[:], 0.0)
+        nc.scalar.activation(warm_out[:], warm_in[:], ACT.Copy)
 
-        load_plane(0, 0)
-        nc.sync.dma_start(list1[:], offs)
-        nc.sync.dma_start(list2[:], offs2)
-        nc.sync.dma_start(out=factor[:], in_=fk.rearrange("(z p t) o -> p z (t o)", z=PASSES, t=PACK))
-        load_w(0)
-        load_plane(0, 1)
-        load_w(1)
-        load_plane(0, 2)
-        for q in range(4):
+        def load_w_scales(q):
             nc.sync.dma_start(
                 out=ws_raw[32 * q : 32 * q + 4].bitcast(I32),
                 in_=w_scales[:, 4 * q : 4 * q + 4, :].rearrange("z r c -> r z c").bitcast(I32),
             )
+
+        load_plane(0, 0)
+        nc.sync.dma_start(list1[:], offs)
+        nc.sync.dma_start(list2[:], offs2)
+        load_plane(0, 1)
+        load_w_scales(0)
+        load_plane(0, 2)
+        load_w_scales(1)
         load_plane(0, 3)
-        for t in range(PACK):
-            load_plane(1, t)
+        load_w_scales(2)
+        load_w_scales(3)
+        load_plane(1, 0)
+        nc.sync.dma_start(out=factor[:], in_=fk.rearrange("(z p t) o -> p z (t o)", z=PASSES, t=PACK))
+        load_plane(1, 1)
+        load_w(0)
+        load_plane(1, 2)
+        load_w(1)
+        load_plane(1, 3)
         nc.sync.dma_start(list3[:], offs3)
         nc.sync.dma_start(out=wb[:].bitcast(I32), in_=wb_words[0].bitcast(I32))
         nc.sync.dma_start(out=res[:], in_=rs)
@@ -105,66 +116,90 @@ def tile_list_largerpicks_relooked_rowpeaks_kernel(
         halves = [slice(h * HALF, (h + 1) * HALF) for h in range(2)]
         entries = [slice(h * HALF // 16, (h + 1) * HALF // 16) for h in range(2)]
 
-        def plane_work(z, t, vector_halves):
+        larger = [keep.tile([P, PACK, J], F32, name=f"larger{z}") for z in range(PASSES)]
+
+        def pick_larger(z, t, second_engine, parts):
             first = keep.tile([P, J], F32, name=f"first{z}{t}")
             second = keep.tile([P, J], F32, name=f"second{z}{t}")
-            larger = keep.tile([P, J], F32, name=f"larger{z}{t}")
-            for h in range(2):
-                gather("scalar", first[:, halves[h]], planes[z][t][:], list1[:, entries[h]])
-                gather("vector" if h < vector_halves else "scalar", second[:, halves[h]], planes[z][t][:], list2[:, entries[h]])
-            for h in range(2):
-                nc.vector.tensor_tensor(larger[:, halves[h]], first[:, halves[h]], second[:, halves[h]], ALU.max)
-                nc.vector.tensor_scalar(u[z][:, halves[h], t], larger[:, halves[h]], factor[:, z, t : t + 1], None, ALU.mult)
+            for cols, ent in parts:
+                gather("scalar", first[:, cols], planes[z][t][:], list1[:, ent])
+                gather(second_engine, second[:, cols], planes[z][t][:], list2[:, ent])
+            for cols, ent in parts:
+                nc.vector.tensor_tensor(larger[z][:, t, cols], first[:, cols], second[:, cols], ALU.max)
 
-        banks = [[psum.tile([P, 2, HALF], F32, name=f"a{h}{d}") for d in range(2)] for h in range(2)]
+        def scale(z, slots, cols):
+            count = slots.stop - slots.start
+            width = cols.stop - cols.start
+            nc.vector.tensor_tensor(
+                u[z][:, cols, slots].rearrange("p (c i) t -> p c t i", i=LINE),
+                larger[z][:, slots, cols].rearrange("p t (c i) -> p c t i", i=LINE),
+                factor[:, z, slots].unsqueeze(1).unsqueeze(3).to_broadcast([P, width // LINE, count, LINE]),
+                ALU.mult,
+            )
+
+        banks0 = [psum.tile([P, 2, HALF], F32, name=f"a0{d}") for d in range(2)]
+        banks1 = [psum.tile([P, HALF], F32, name=f"a1{t}") for t in range(PACK)]
 
         def first_stage(z, h):
             for t in range(PACK):
                 rows = slice(t * P, (t + 1) * P)
                 nc.tensor.matmul_mx(
-                    out=banks[h][t // 2][:, t % 2, :],
+                    out=banks0[t // 2][:, t % 2, :] if h == 0 else banks1[t][:],
                     lhsT=w_codes[z][:, rows].bitcast(E5M2X4),
                     lhsT_scale=ws[:, z, rows],
                     rhs=u_codes[z][:, halves[h]].bitcast(E5M2X4),
                     rhs_scale=u_scales[z][:, halves[h]],
-                    start=(z == 0 and t % 2 == 0),
-                    stop=(z == PASSES - 1 and t % 2 == 1),
+                    start=(z == 0 and (h == 1 or t % 2 == 0)),
+                    stop=(z == PASSES - 1 and (h == 1 or t % 2 == 1)),
                 )
 
-        plane_work(0, 0, 2)
-        deal_w(0)
-        plane_work(0, 1, 1)
-        deal_w(1)
-        plane_work(0, 2, 0)
+        whole = [(slice(0, J), slice(0, J // 16))]
+        pick_larger(0, 0, "vector", whole)
+        pick_larger(0, 1, "vector", whole)
+        pick_larger(0, 2, "scalar", whole)
         nc.vector.tensor_copy(
             out=ws[:].rearrange("p z (t m) -> p z t m", t=PACK),
             in_=ws_raw[:].rearrange("p z (m t) -> p z t m", t=PACK),
         )
-        plane_work(0, 3, 1)
+        pick_larger(0, 3, "vector", whole)
+        scale(0, slice(0, PACK), slice(0, J))
+        pick_larger(1, 0, "scalar", whole)
         quantise_u(0, slice(0, J))
+        deal_w(0)
         for h in range(2):
             first_stage(0, h)
-        plane_work(1, 0, 0)
-        for t in range(1, PACK):
-            plane_work(1, t, 1)
-        for h in range(2):
-            quantise_u(1, halves[h])
+        pick_larger(1, 1, "scalar", whole)
+        deal_w(1)
+        pick_larger(1, 2, "scalar", whole)
+        pick_larger(1, 3, "vector", list(zip(halves, entries)))
+        scale(1, slice(0, PACK), halves[0])
+        scale(1, slice(0, PACK), slice(HALF, HALF + HALF // 2))
+        quantise_u(1, halves[0])
+        scale(1, slice(0, PACK), slice(HALF + HALF // 2, J))
+        quantise_u(1, halves[1])
 
         res3 = keep.tile([P, N], F32, name="res3")
         nc.scalar.activation(res3[:], res[:], ACT.Copy, scale=0.3)
 
-        ha = [keep.tile([P, 2, J], F32, name=f"ha{d}") for d in range(2)]
-        for h in range(2):
-            first_stage(1, h)
-            for d in range(2):
-                if h == 0 and d == 1:
-                    nc.vector.tensor_scalar(ha[d][:, :, halves[h]], banks[h][d][:], 0.0, None, ALU.max)
-                else:
-                    nc.scalar.activation(ha[d][:, :, halves[h]], banks[h][d][:], ACT.Relu)
+        ha = keep.tile([P, PACK, J], F32, name="ha")
+
+        def relu(engine, dst, src):
+            if engine == "scalar":
+                nc.scalar.activation(dst, src, ACT.Relu)
+            else:
+                nc.vector.tensor_scalar(dst, src, 0.0, None, ALU.max)
+
+        engines = ("scalar", "vector")
+        first_stage(1, 0)
+        for d in range(2):
+            relu(engines[d], ha[:, 2 * d : 2 * d + 2, halves[0]], banks0[d][:])
+        first_stage(1, 1)
+        for t in range(PACK):
+            relu(engines[t % 2], ha[:, t, halves[1]], banks1[t][:])
 
         hid32 = keep.tile([P, PACK, O], F32, name="hid32")
         for t in range(PACK):
-            gather("scalar" if t == PACK - 1 else "vector", hid32[:, t, :], ha[t // 2][:, t % 2, :], list3[:])
+            gather(engines[t % 2], hid32[:, t, :], ha[:, t, :], list3[:])
 
         hid = keep.tile([P, O, PACK], BF16, name="hid", align_bytes=64)
         h_codes = keep.tile([P, O], I32, name="h_codes", align_bytes=64)

@@ -77,10 +77,10 @@ def tile_list_largerpicks_relooked_rowpeaks_kernel(
         load_plane(1, 0)
         nc.sync.dma_start(out=factor[:], in_=fk.rearrange("(z p t) o -> p z (t o)", z=PASSES, t=PACK))
         load_plane(1, 1)
-        load_w(0)
         load_plane(1, 2)
-        load_w(1)
+        load_w(0)
         load_plane(1, 3)
+        load_w(1)
         nc.sync.dma_start(list3[:], offs3)
         nc.sync.dma_start(out=wb[:].bitcast(I32), in_=wb_words[0].bitcast(I32))
         nc.sync.dma_start(out=res[:], in_=rs)
@@ -158,25 +158,24 @@ def tile_list_largerpicks_relooked_rowpeaks_kernel(
         pick_larger(0, 1, "vector", whole)
         pick_larger(0, 2, "scalar", whole)
         nc.vector.tensor_copy(
-            out=ws[:].rearrange("p z (t m) -> p z t m", t=PACK),
-            in_=ws_raw[:].rearrange("p z (m t) -> p z t m", t=PACK),
+            out=ws[:].rearrange("p z (t c i) -> p z c t i", t=PACK, i=16),
+            in_=ws_raw[:].rearrange("p z (c i t) -> p z c t i", t=PACK, i=16),
         )
         pick_larger(0, 3, "vector", whole)
         scale(0, slice(0, PACK), slice(0, J))
         pick_larger(1, 0, "scalar", whole)
         quantise_u(0, slice(0, J))
+        pick_larger(1, 1, "scalar", whole)
+        pick_larger(1, 2, "vector", whole)
         deal_w(0)
         for h in range(2):
             first_stage(0, h)
-        pick_larger(1, 1, "scalar", whole)
-        deal_w(1)
-        pick_larger(1, 2, "scalar", whole)
         pick_larger(1, 3, "vector", list(zip(halves, entries)))
-        scale(1, slice(0, PACK), halves[0])
-        scale(1, slice(0, PACK), slice(HALF, HALF + HALF // 2))
-        quantise_u(1, halves[0])
-        scale(1, slice(0, PACK), slice(HALF + HALF // 2, J))
-        quantise_u(1, halves[1])
+        for h in range(2):
+            scale(1, slice(0, PACK), halves[h])
+        deal_w(1)
+        for h in range(2):
+            quantise_u(1, halves[h])
 
         res3 = keep.tile([P, N], F32, name="res3")
         nc.scalar.activation(res3[:], res[:], ACT.Copy, scale=0.3)

@@ -18,8 +18,12 @@ ACT = mybir.ActivationFunctionType
 P = 128
 PACK = 4
 PASSES = K // (P * PACK)
+QUADRANTS = 4
+PER_COLUMN = 16
 HALF = J // 2
-LINE = 4
+LINE_BYTES = 16
+LINE = LINE_BYTES // 4
+ENGINES = ("scalar", "vector")
 
 
 def tile_list_largerpicks_relooked_rowpeaks_kernel(
@@ -30,9 +34,9 @@ def tile_list_largerpicks_relooked_rowpeaks_kernel(
         keep = ctx.enter_context(tc.tile_pool(name="keep", bufs=1))
         psum = ctx.enter_context(tc.psum_pool(name="psum", bufs=1))
 
-        list1 = keep.tile([P, J // 16], U16, name="list1")
-        list2 = keep.tile([P, J // 16], U16, name="list2")
-        list3 = keep.tile([P, O // 16], U16, name="list3")
+        list1 = keep.tile([P, J // PER_COLUMN], U16, name="list1")
+        list2 = keep.tile([P, J // PER_COLUMN], U16, name="list2")
+        list3 = keep.tile([P, O // PER_COLUMN], U16, name="list3")
         planes = [[keep.tile([P, T], F32, name=f"x{z}{t}") for t in range(PACK)] for z in range(PASSES)]
         factor = keep.tile([P, PASSES, PACK], F32, name="factor")
         w_raw = [keep.tile([P, R], I32, name=f"w_raw{z}") for z in range(PASSES)]
@@ -43,20 +47,21 @@ def tile_list_largerpicks_relooked_rowpeaks_kernel(
         wbs = keep.tile([P, N], U8, name="wbs", align_bytes=64)
         res = keep.tile([P, N], F32, name="res")
 
-        xv = xf.rearrange("(z p t) c -> z t p c", z=PASSES, t=PACK)
-
-        def load_plane(z, t):
-            nc.sync.dma_start(out=planes[z][t][:], in_=xv[z, t])
-
-        def load_w(z):
-            nc.sync.dma_start(out=w_raw[z][:], in_=w_words[z].rearrange("p c t -> p (c t)").bitcast(I32))
-
         nc.gpsimd.memset(ws_raw[:].rearrange("p z c -> p (z c)").bitcast(I32), 0)
         nc.gpsimd.memset(wbs[:].bitcast(I32), 0)
+
         warm_in = keep.tile([P, 1], F32, name="warm_in")
         warm_out = keep.tile([P, 1], F32, name="warm_out")
         nc.vector.memset(warm_in[:], 0.0)
         nc.scalar.activation(warm_out[:], warm_in[:], ACT.Copy)
+
+        xf_planes = xf.rearrange("(z p t) c -> z t p c", z=PASSES, t=PACK)
+
+        def load_plane(z, t):
+            nc.sync.dma_start(out=planes[z][t][:], in_=xf_planes[z, t])
+
+        def load_w(z):
+            nc.sync.dma_start(out=w_raw[z][:], in_=w_words[z].rearrange("p c t -> p (c t)").bitcast(I32))
 
         def load_w_scales(q):
             nc.sync.dma_start(
@@ -84,7 +89,7 @@ def tile_list_largerpicks_relooked_rowpeaks_kernel(
         nc.sync.dma_start(list3[:], offs3)
         nc.sync.dma_start(out=wb[:].bitcast(I32), in_=wb_words[0].bitcast(I32))
         nc.sync.dma_start(out=res[:], in_=rs)
-        for q in range(4):
+        for q in range(QUADRANTS):
             nc.sync.dma_start(
                 out=wbs[32 * q : 32 * q + 4].bitcast(I32),
                 in_=wb_scales[0, 4 * q : 4 * q + 4, :].bitcast(I32),
@@ -102,80 +107,85 @@ def tile_list_largerpicks_relooked_rowpeaks_kernel(
                 in_=w_raw[z][:].rearrange("p (c i t) -> p c t i", t=PACK, i=LINE),
             )
 
+        def deal_w_scales():
+            nc.vector.tensor_copy(
+                out=ws[:].rearrange("p z (t c i) -> p z c t i", t=PACK, i=LINE_BYTES),
+                in_=ws_raw[:].rearrange("p z (c i t) -> p z c t i", t=PACK, i=LINE_BYTES),
+            )
+
         u = [keep.tile([P, J, PACK], BF16, name=f"u{z}", align_bytes=64) for z in range(PASSES)]
         u_codes = [keep.tile([P, J], I32, name=f"u_codes{z}", align_bytes=64) for z in range(PASSES)]
         u_scales = [keep.tile([P, J], U8, name=f"u_scales{z}", align_bytes=64) for z in range(PASSES)]
 
-        def quantise_u(z, cols):
+        def quantise_u(z, slots):
             nc.vector.quantize_mx(
-                out=u_codes[z][:, cols].bitcast(E5M2X4),
-                scales=u_scales[z][:, cols],
-                in_=u[z][:, cols, :].rearrange("p j t -> p (j t)"),
+                out=u_codes[z][:, slots].bitcast(E5M2X4),
+                scales=u_scales[z][:, slots],
+                in_=u[z][:, slots, :].rearrange("p j t -> p (j t)"),
             )
 
+        all_slots = slice(0, J)
         halves = [slice(h * HALF, (h + 1) * HALF) for h in range(2)]
-        entries = [slice(h * HALF // 16, (h + 1) * HALF // 16) for h in range(2)]
 
         larger = [keep.tile([P, PACK, J], F32, name=f"larger{z}") for z in range(PASSES)]
 
         def pick_larger(z, t, second_engine, parts):
             first = keep.tile([P, J], F32, name=f"first{z}{t}")
             second = keep.tile([P, J], F32, name=f"second{z}{t}")
-            for cols, ent in parts:
-                gather("scalar", first[:, cols], planes[z][t][:], list1[:, ent])
-                gather(second_engine, second[:, cols], planes[z][t][:], list2[:, ent])
-            for cols, ent in parts:
-                nc.vector.tensor_tensor(larger[z][:, t, cols], first[:, cols], second[:, cols], ALU.max)
+            for slots in parts:
+                entries = slice(slots.start // PER_COLUMN, slots.stop // PER_COLUMN)
+                gather("scalar", first[:, slots], planes[z][t][:], list1[:, entries])
+                gather(second_engine, second[:, slots], planes[z][t][:], list2[:, entries])
+            for slots in parts:
+                nc.vector.tensor_tensor(larger[z][:, t, slots], first[:, slots], second[:, slots], ALU.max)
 
-        def scale(z, slots, cols):
-            count = slots.stop - slots.start
-            width = cols.stop - cols.start
+        def scale(z, slots):
+            runs = (slots.stop - slots.start) // LINE
             nc.vector.tensor_tensor(
-                u[z][:, cols, slots].rearrange("p (c i) t -> p c t i", i=LINE),
-                larger[z][:, slots, cols].rearrange("p t (c i) -> p c t i", i=LINE),
-                factor[:, z, slots].unsqueeze(1).unsqueeze(3).to_broadcast([P, width // LINE, count, LINE]),
+                u[z][:, slots, :].rearrange("p (c i) t -> p c t i", i=LINE),
+                larger[z][:, :, slots].rearrange("p t (c i) -> p c t i", i=LINE),
+                factor[:, z, :].unsqueeze(1).unsqueeze(3).to_broadcast([P, runs, PACK, LINE]),
                 ALU.mult,
             )
 
-        banks0 = [psum.tile([P, 2, HALF], F32, name=f"a0{d}") for d in range(2)]
+        banks0 = [psum.tile([P, 2, HALF], F32, name=f"a0{d}") for d in range(PACK // 2)]
         banks1 = [psum.tile([P, HALF], F32, name=f"a1{t}") for t in range(PACK)]
 
         def first_stage(z, h):
             for t in range(PACK):
                 rows = slice(t * P, (t + 1) * P)
+                first_in_bank = h == 1 or t % 2 == 0
+                last_in_bank = h == 1 or t % 2 == 1
                 nc.tensor.matmul_mx(
                     out=banks0[t // 2][:, t % 2, :] if h == 0 else banks1[t][:],
                     lhsT=w_codes[z][:, rows].bitcast(E5M2X4),
                     lhsT_scale=ws[:, z, rows],
                     rhs=u_codes[z][:, halves[h]].bitcast(E5M2X4),
                     rhs_scale=u_scales[z][:, halves[h]],
-                    start=(z == 0 and (h == 1 or t % 2 == 0)),
-                    stop=(z == PASSES - 1 and (h == 1 or t % 2 == 1)),
+                    start=(z == 0 and first_in_bank),
+                    stop=(z == PASSES - 1 and last_in_bank),
                 )
 
-        whole = [(slice(0, J), slice(0, J // 16))]
-        pick_larger(0, 0, "vector", whole)
-        pick_larger(0, 1, "vector", whole)
-        pick_larger(0, 2, "scalar", whole)
-        nc.vector.tensor_copy(
-            out=ws[:].rearrange("p z (t c i) -> p z c t i", t=PACK, i=16),
-            in_=ws_raw[:].rearrange("p z (c i t) -> p z c t i", t=PACK, i=16),
-        )
-        pick_larger(0, 3, "vector", whole)
-        scale(0, slice(0, PACK), slice(0, J))
-        pick_larger(1, 0, "scalar", whole)
-        quantise_u(0, slice(0, J))
-        pick_larger(1, 1, "scalar", whole)
-        pick_larger(1, 2, "vector", whole)
+        pick_larger(0, 0, "vector", [all_slots])
+        pick_larger(0, 1, "vector", [all_slots])
+        pick_larger(0, 2, "vector", [all_slots])
+        deal_w_scales()
+        pick_larger(0, 3, "vector", [all_slots])
+        scale(0, all_slots)
+        pick_larger(1, 0, "scalar", [all_slots])
+        quantise_u(0, all_slots)
+        pick_larger(1, 1, "scalar", [all_slots])
+        pick_larger(1, 2, "vector", [all_slots])
         deal_w(0)
         for h in range(2):
             first_stage(0, h)
-        pick_larger(1, 3, "vector", list(zip(halves, entries)))
-        for h in range(2):
-            scale(1, slice(0, PACK), halves[h])
+
+        pick_larger(1, 3, "vector", halves)
+        for slots in halves:
+            scale(1, slots)
         deal_w(1)
-        for h in range(2):
-            quantise_u(1, halves[h])
+        for slots in halves:
+            quantise_u(1, slots)
 
         res3 = keep.tile([P, N], F32, name="res3")
         nc.scalar.activation(res3[:], res[:], ACT.Copy, scale=0.3)
@@ -188,32 +198,31 @@ def tile_list_largerpicks_relooked_rowpeaks_kernel(
             else:
                 nc.vector.tensor_scalar(dst, src, 0.0, None, ALU.max)
 
-        engines = ("scalar", "vector")
         first_stage(1, 0)
-        for d in range(2):
-            relu(engines[d], ha[:, 2 * d : 2 * d + 2, halves[0]], banks0[d][:])
+        for d in range(PACK // 2):
+            relu(ENGINES[d], ha[:, 2 * d : 2 * d + 2, halves[0]], banks0[d][:])
         first_stage(1, 1)
         for t in range(PACK):
-            relu(engines[t % 2], ha[:, t, halves[1]], banks1[t][:])
+            relu(ENGINES[t % 2], ha[:, t, halves[1]], banks1[t][:])
 
         hid32 = keep.tile([P, PACK, O], F32, name="hid32")
         for t in range(PACK):
-            gather(engines[t % 2], hid32[:, t, :], ha[:, t, :], list3[:])
+            gather(ENGINES[t % 2], hid32[:, t, :], ha[:, t, :], list3[:])
 
         hid = keep.tile([P, O, PACK], BF16, name="hid", align_bytes=64)
         h_codes = keep.tile([P, O], I32, name="h_codes", align_bytes=64)
         h_scales = keep.tile([P, O], U8, name="h_scales", align_bytes=64)
-        places = [slice(h * O // 2, (h + 1) * O // 2) for h in range(2)]
-        for s in places:
+        place_halves = [slice(0, O // 2), slice(O // 2, O)]
+        for places in place_halves:
             nc.vector.tensor_copy(
-                out=hid[:, s, :].rearrange("p (c i) t -> p c t i", i=LINE),
-                in_=hid32[:, :, s].rearrange("p t (c i) -> p c t i", i=LINE),
+                out=hid[:, places, :].rearrange("p (c i) t -> p c t i", i=LINE),
+                in_=hid32[:, :, places].rearrange("p t (c i) -> p c t i", i=LINE),
             )
-        for s in places:
+        for places in place_halves:
             nc.vector.quantize_mx(
-                out=h_codes[:, s].bitcast(E5M2X4),
-                scales=h_scales[:, s],
-                in_=hid[:, s, :].rearrange("p o t -> p (o t)"),
+                out=h_codes[:, places].bitcast(E5M2X4),
+                scales=h_scales[:, places],
+                in_=hid[:, places, :].rearrange("p o t -> p (o t)"),
             )
 
         prod = psum.tile([P, N], F32, name="prod")
@@ -229,11 +238,11 @@ def tile_list_largerpicks_relooked_rowpeaks_kernel(
 
         size = keep.tile([P, N], F32, name="size")
         shifted = keep.tile([P, N], F32, name="shifted")
-        peak = keep.tile([P, 1], F32, name="peak")
+        divisor = keep.tile([P, 1], F32, name="peak")
         inverse = keep.tile([P, 1], F32, name="inverse")
         result = keep.tile([P, N], F32, name="result")
         nc.scalar.activation(size[:], prod[:], ACT.Abs)
-        nc.vector.tensor_scalar(shifted[:], size[:], 0.2, None, ALU.add, ALU.max, accum_out=peak[:])
-        nc.vector.reciprocal(inverse[:], peak[:])
+        nc.vector.tensor_scalar(shifted[:], size[:], 0.2, None, ALU.add, ALU.max, accum_out=divisor[:])
+        nc.vector.reciprocal(inverse[:], divisor[:])
         nc.vector.scalar_tensor_tensor(result[:], prod[:], inverse[:], res3[:], ALU.mult, ALU.add)
         nc.sync.dma_start(out=out, in_=result[:])

from contextlib import ExitStack

import concourse.mybir as mybir

K, T, J, R, O, N = 1024, 1024, 256, 512, 128, 256
FLOPS = 2 * K * R * J + 2 * R * O * N

F32 = mybir.dt.float32
BF16 = mybir.dt.bfloat16
I32 = mybir.dt.int32
U16 = mybir.dt.uint16
U8 = mybir.dt.uint8
E5M2X4 = mybir.dt.float8_e5m2_x4
E2M1X4 = mybir.dt.float4_e2m1fn_x4
ALU = mybir.AluOpType
ACT = mybir.ActivationFunctionType

P = 128
PACK = 4
PASSES = K // (P * PACK)
QUADRANTS = 4
PER_COLUMN = 16
HALF = J // 2
LINE_BYTES = 16
LINE = LINE_BYTES // 4
ENGINES = ("scalar", "vector")


def tile_list_largerpicks_relooked_rowpeaks_kernel(
    tc, xf, fk, w_words, w_scales, wb_words, wb_scales, rs, offs, offs2, offs3, out
):
    nc = tc.nc
    with ExitStack() as ctx:
        keep = ctx.enter_context(tc.tile_pool(name="keep", bufs=1))
        psum = ctx.enter_context(tc.psum_pool(name="psum", bufs=1))

        list1 = keep.tile([P, J // PER_COLUMN], U16, name="list1")
        list2 = keep.tile([P, J // PER_COLUMN], U16, name="list2")
        list3 = keep.tile([P, O // PER_COLUMN], U16, name="list3")
        planes = [[keep.tile([P, T], F32, name=f"x{z}{t}") for t in range(PACK)] for z in range(PASSES)]
        factor = keep.tile([P, PASSES, PACK], F32, name="factor")
        w_raw = [keep.tile([P, R], I32, name=f"w_raw{z}") for z in range(PASSES)]
        w_codes = [keep.tile([P, R], I32, name=f"w_codes{z}", align_bytes=64) for z in range(PASSES)]
        ws_raw = keep.tile([P, PASSES, R], U8, name="ws_raw")
        ws = keep.tile([P, PASSES, R], U8, name="ws", align_bytes=64)
        wb = keep.tile([P, 2 * N], U8, name="wb", align_bytes=64)
        wbs = keep.tile([P, N], U8, name="wbs", align_bytes=64)
        res = keep.tile([P, N], F32, name="res")

        nc.gpsimd.memset(ws_raw[:].rearrange("p z c -> p (z c)").bitcast(I32), 0)
        nc.gpsimd.memset(wbs[:].bitcast(I32), 0)

        warm_in = keep.tile([P, 1], F32, name="warm_in")
        warm_out = keep.tile([P, 1], F32, name="warm_out")
        nc.vector.memset(warm_in[:], 0.0)
        nc.scalar.activation(warm_out[:], warm_in[:], ACT.Copy)

        xf_planes = xf.rearrange("(z p t) c -> z t p c", z=PASSES, t=PACK)

        def load_plane(z, t):
            nc.sync.dma_start(out=planes[z][t][:], in_=xf_planes[z, t])

        def load_w(z):
            nc.sync.dma_start(out=w_raw[z][:], in_=w_words[z].rearrange("p c t -> p (c t)").bitcast(I32))

        def load_w_scales(q):
            nc.sync.dma_start(
                out=ws_raw[32 * q : 32 * q + 4].bitcast(I32),
                in_=w_scales[:, 4 * q : 4 * q + 4, :].rearrange("z r c -> r z c").bitcast(I32),
            )

        load_plane(0, 0)
        nc.sync.dma_start(list1[:], offs)
        nc.sync.dma_start(list2[:], offs2)
        load_plane(0, 1)
        load_w_scales(0)
        load_plane(0, 2)
        load_w_scales(1)
        load_plane(0, 3)
        load_w_scales(2)
        load_w_scales(3)
        load_plane(1, 0)
        nc.sync.dma_start(out=factor[:], in_=fk.rearrange("(z p t) o -> p z (t o)", z=PASSES, t=PACK))
        load_plane(1, 1)
        load_plane(1, 2)
        load_w(0)
        load_plane(1, 3)
        load_w(1)
        nc.sync.dma_start(list3[:], offs3)
        nc.sync.dma_start(out=wb[:].bitcast(I32), in_=wb_words[0].bitcast(I32))
        nc.sync.dma_start(out=res[:], in_=rs)
        for q in range(QUADRANTS):
            nc.sync.dma_start(
                out=wbs[32 * q : 32 * q + 4].bitcast(I32),
                in_=wb_scales[0, 4 * q : 4 * q + 4, :].bitcast(I32),
            )

        def gather(engine, dst, window, offsets):
            if engine == "scalar":
                nc.scalar.activation(dst, window.indirect(offsets), ACT.Copy)
            else:
                nc.vector.tensor_copy(dst, window.indirect(offsets))

        def deal_w(z):
            nc.vector.tensor_copy(
                out=w_codes[z][:].rearrange("p (t c i) -> p c t i", t=PACK, i=LINE),
                in_=w_raw[z][:].rearrange("p (c i t) -> p c t i", t=PACK, i=LINE),
            )

        def deal_w_scales():
            nc.vector.tensor_copy(
                out=ws[:].rearrange("p z (t c i) -> p z c t i", t=PACK, i=LINE_BYTES),
                in_=ws_raw[:].rearrange("p z (c i t) -> p z c t i", t=PACK, i=LINE_BYTES),
            )

        u = [keep.tile([P, J, PACK], BF16, name=f"u{z}", align_bytes=64) for z in range(PASSES)]
        u_codes = [keep.tile([P, J], I32, name=f"u_codes{z}", align_bytes=64) for z in range(PASSES)]
        u_scales = [keep.tile([P, J], U8, name=f"u_scales{z}", align_bytes=64) for z in range(PASSES)]

        def quantise_u(z, slots):
            nc.vector.quantize_mx(
                out=u_codes[z][:, slots].bitcast(E5M2X4),
                scales=u_scales[z][:, slots],
                in_=u[z][:, slots, :].rearrange("p j t -> p (j t)"),
            )

        all_slots = slice(0, J)
        halves = [slice(h * HALF, (h + 1) * HALF) for h in range(2)]

        larger = [keep.tile([P, PACK, J], F32, name=f"larger{z}") for z in range(PASSES)]

        def pick_larger(z, t, second_engine, parts):
            first = keep.tile([P, J], F32, name=f"first{z}{t}")
            second = keep.tile([P, J], F32, name=f"second{z}{t}")
            for slots in parts:
                entries = slice(slots.start // PER_COLUMN, slots.stop // PER_COLUMN)
                gather("scalar", first[:, slots], planes[z][t][:], list1[:, entries])
                gather(second_engine, second[:, slots], planes[z][t][:], list2[:, entries])
            for slots in parts:
                nc.vector.tensor_tensor(larger[z][:, t, slots], first[:, slots], second[:, slots], ALU.max)

        def scale(z, slots):
            runs = (slots.stop - slots.start) // LINE
            nc.vector.tensor_tensor(
                u[z][:, slots, :].rearrange("p (c i) t -> p c t i", i=LINE),
                larger[z][:, :, slots].rearrange("p t (c i) -> p c t i", i=LINE),
                factor[:, z, :].unsqueeze(1).unsqueeze(3).to_broadcast([P, runs, PACK, LINE]),
                ALU.mult,
            )

        banks0 = [psum.tile([P, 2, HALF], F32, name=f"a0{d}") for d in range(PACK // 2)]
        banks1 = [psum.tile([P, HALF], F32, name=f"a1{t}") for t in range(PACK)]

        def first_stage(z, h):
            for t in range(PACK):
                rows = slice(t * P, (t + 1) * P)
                first_in_bank = h == 1 or t % 2 == 0
                last_in_bank = h == 1 or t % 2 == 1
                nc.tensor.matmul_mx(
                    out=banks0[t // 2][:, t % 2, :] if h == 0 else banks1[t][:],
                    lhsT=w_codes[z][:, rows].bitcast(E5M2X4),
                    lhsT_scale=ws[:, z, rows],
                    rhs=u_codes[z][:, halves[h]].bitcast(E5M2X4),
                    rhs_scale=u_scales[z][:, halves[h]],
                    start=(z == 0 and first_in_bank),
                    stop=(z == PASSES - 1 and last_in_bank),
                )

        pick_larger(0, 0, "vector", [all_slots])
        pick_larger(0, 1, "vector", [all_slots])
        pick_larger(0, 2, "vector", [all_slots])
        deal_w_scales()
        pick_larger(0, 3, "vector", [all_slots])
        scale(0, all_slots)
        pick_larger(1, 0, "scalar", [all_slots])
        quantise_u(0, all_slots)
        pick_larger(1, 1, "scalar", [all_slots])
        pick_larger(1, 2, "vector", [all_slots])
        deal_w(0)
        for h in range(2):
            first_stage(0, h)

        pick_larger(1, 3, "vector", halves)
        for slots in halves:
            scale(1, slots)
        deal_w(1)
        for slots in halves:
            quantise_u(1, slots)

        res3 = keep.tile([P, N], F32, name="res3")
        nc.scalar.activation(res3[:], res[:], ACT.Copy, scale=0.3)

        ha = keep.tile([P, PACK, J], F32, name="ha")

        def relu(engine, dst, src):
            if engine == "scalar":
                nc.scalar.activation(dst, src, ACT.Relu)
            else:
                nc.vector.tensor_scalar(dst, src, 0.0, None, ALU.max)

        first_stage(1, 0)
        for d in range(PACK // 2):
            relu(ENGINES[d], ha[:, 2 * d : 2 * d + 2, halves[0]], banks0[d][:])
        first_stage(1, 1)
        for t in range(PACK):
            relu(ENGINES[t % 2], ha[:, t, halves[1]], banks1[t][:])

        hid32 = keep.tile([P, PACK, O], F32, name="hid32")
        for t in range(PACK):
            gather(ENGINES[t % 2], hid32[:, t, :], ha[:, t, :], list3[:])

        hid = keep.tile([P, O, PACK], BF16, name="hid", align_bytes=64)
        h_codes = keep.tile([P, O], I32, name="h_codes", align_bytes=64)
        h_scales = keep.tile([P, O], U8, name="h_scales", align_bytes=64)
        place_halves = [slice(0, O // 2), slice(O // 2, O)]
        for places in place_halves:
            nc.vector.tensor_copy(
                out=hid[:, places, :].rearrange("p (c i) t -> p c t i", i=LINE),
                in_=hid32[:, :, places].rearrange("p t (c i) -> p c t i", i=LINE),
            )
        for places in place_halves:
            nc.vector.quantize_mx(
                out=h_codes[:, places].bitcast(E5M2X4),
                scales=h_scales[:, places],
                in_=hid[:, places, :].rearrange("p o t -> p (o t)"),
            )

        prod = psum.tile([P, N], F32, name="prod")
        nc.tensor.matmul_mx(
            out=prod[:],
            lhsT=h_codes[:].bitcast(E5M2X4),
            lhsT_scale=h_scales[:],
            rhs=wb[:].bitcast(E2M1X4),
            rhs_scale=wbs[:],
            start=True,
            stop=True,
        )

        size = keep.tile([P, N], F32, name="size")
        shifted = keep.tile([P, N], F32, name="shifted")
        divisor = keep.tile([P, 1], F32, name="peak")
        inverse = keep.tile([P, 1], F32, name="inverse")
        result = keep.tile([P, N], F32, name="result")
        nc.scalar.activation(size[:], prod[:], ACT.Abs)
        nc.vector.tensor_scalar(shifted[:], size[:], 0.2, None, ALU.add, ALU.max, accum_out=divisor[:])
        nc.vector.reciprocal(inverse[:], divisor[:])
        nc.vector.scalar_tensor_tensor(result[:], prod[:], inverse[:], res3[:], ALU.mult, ALU.add)
        nc.sync.dma_start(out=out, in_=result[:])
